import numpy as np
import ml_dtypes


def mxq(x, axis, fmt="e4m3"):
    dtype, down = {"e4m3": (ml_dtypes.float8_e4m3fn, 7), "e5m2": (ml_dtypes.float8_e5m2, 14)}[fmt]
    v = np.moveaxis(np.asarray(x, np.float32).astype(ml_dtypes.bfloat16).astype(np.float64), axis, -1)
    blocks = v.reshape(v.shape[:-1] + (-1, 32))
    amax = np.abs(blocks).max(-1, keepdims=True)
    byte = np.maximum(np.where(amax > 0, np.frexp(amax)[1] - 1 + 127, 0) - down, 1)
    scale = np.exp2(byte - 127.0)
    codes = (blocks / scale).astype(np.float32).astype(dtype).astype(np.float64)
    return np.moveaxis((codes * scale).reshape(v.shape), -1, axis)


WIDE = False


def mx_kscale(k):
    if not WIDE:
        return np.ones(k)
    levels = np.array([30, -30])
    if k % 512:
        return np.exp2(np.random.permutation(np.resize(levels, k // 32))).repeat(32)
    a = np.empty((k // 512, 16))
    for p in range(k // 512):
        a[p, :8] = np.random.permutation(np.resize(levels, 8))
        for g in range(8):
            far = levels[np.abs(levels - a[p, g]) >= 10]
            a[p, g + 8] = far[np.random.randint(len(far))]
    return np.exp2(a.ravel()).repeat(32)


def f64(x):
    return np.asarray(x).astype(np.float64)


def striped(idx):
    return np.tile(np.asarray(idx).reshape(-1, 16).T, (8, 1)).astype(np.uint16)


def unstriped(offs):
    return offs[:16].T.reshape(-1).astype(np.int64)


E2M1 = np.array([0.0, 0.5, 1.0, 1.5, 2.0, 3.0, 4.0, 6.0, -0.0, -0.5, -1.0, -1.5, -2.0, -3.0, -4.0, -6.0])


def pack_weight(w, fmt):
    k, n = w.shape
    w = f64(np.asarray(w, np.float32).astype(ml_dtypes.bfloat16)).reshape(k // 32, 32, n)
    amax = np.abs(w).max(1)
    if fmt == "e4m3":
        byte = np.frexp(amax)[1] - 1 + 127 - 7
    else:
        mant, ex = np.frexp(amax / 6.0)
        byte = np.where(mant > 0.5, ex, ex - 1) + 127
    byte = np.clip(np.where(amax > 0, byte, 1), 1, 254)
    scaled = (w * np.exp2(127.0 - byte)[:, None, :]).reshape(k, n).astype(np.float32)
    by_word = np.ascontiguousarray(scaled.reshape(k // 512, 128, 4, n).transpose(0, 1, 3, 2))
    if fmt == "e4m3":
        words = by_word.astype(ml_dtypes.float8_e4m3fn).view(np.uint8)
    else:
        c = by_word.astype(ml_dtypes.float4_e2m1fn).view(np.uint8) & 0xF
        words = (c[..., 0::2] | (c[..., 1::2] << 4)).reshape(k // 512, 128, 2 * n)
    return np.ascontiguousarray(words), np.ascontiguousarray(byte.astype(np.uint8).reshape(k // 512, 16, n))


def unpack_weight(words, scales, fmt):
    g, _, n = scales.shape
    words = np.ascontiguousarray(words).reshape(g, 128, n, -1)
    if fmt == "e4m3":
        vals = words.view(ml_dtypes.float8_e4m3fn).astype(np.float64)
    else:
        nib = np.empty((g, 128, n, 4), np.uint8)
        nib[..., 0::2] = words & 0xF
        nib[..., 1::2] = words >> 4
        vals = E2M1[nib]
    vals = vals * np.repeat(np.exp2(scales.astype(np.float64) - 127.0), 8, axis=1)[..., None]
    return vals.transpose(0, 1, 3, 2).reshape(g * 512, n)


def bf(x):
    return np.asarray(x, np.float32).astype(ml_dtypes.bfloat16)


def planes(Y):
    r, m = Y.shape
    b = f64(bf(Y)).reshape(r // 32, 32, m)
    amax = np.abs(b).max(1)
    byte = np.clip(np.where(amax > 0, np.frexp(amax)[1] - 1 + 127 - 7, 1), 1, 254)
    codes = (b * np.exp2(127.0 - byte)[:, None, :]).reshape(r, m).astype(np.float32).astype(ml_dtypes.float8_e4m3fn).view(np.uint8)
    words = codes.reshape(r // 512, 128, 4, m).transpose(0, 1, 3, 2)
    return np.ascontiguousarray(words), np.ascontiguousarray(byte.astype(np.uint8).reshape(r // 512, 16, m))


K, T, J, S, R, N, C = 512, 512, 256, 512, 512, 512, 1024


def setup_inputs():
    n = np.random.standard_normal
    idx = np.random.permutation(T)[:J]
    idx2 = np.random.permutation(S)[:J]
    idx3 = np.random.permutation(C)[:J]
    fk = mx_kscale(K)
    fr = mx_kscale(R)
    wp = pack_weight(n((K, R)) * 1 / np.sqrt(K) * fk[:, None], "e4m3")
    wbp = pack_weight(n((R, N)) * 1 / np.sqrt(R) / fr[:, None], "e2m1")
    return {
        "xa": (n((K, T))).astype(np.float32),
        "xb": (n((K, S))).astype(np.float32),
        "fk": (np.random.uniform(0.5, 2.0, (K, 1)) / fk[:, None]).astype(np.float32),
        "w_words": wp[0],
        "w_scales": wp[1],
        "us": (np.random.uniform(0.5, 1.5, (1, R)) * fr).astype(np.float32),
        "wb_words": wbp[0],
        "wb_scales": wbp[1],
        "old": (1.0 * n((N, C))).astype(np.float32),
        "offs": striped(idx),
        "offs2": striped(idx2),
        "offs3": striped(idx3),
    }


def reference(xa, xb, fk, w_words, w_scales, us, wb_words, wb_scales, old, offs, offs2, offs3):
    idx = unstriped(offs)
    idx2 = unstriped(offs2)
    idx3 = unstriped(offs3)
    wu = unpack_weight(w_words, w_scales, "e4m3")
    wbu = unpack_weight(wb_words, wb_scales, "e2m1")
    u = f64(xa)[:, idx] * f64(xb)[:, idx2] * f64(fk)
    uq = mxq(u, 0, "e4m3")
    a = uq.T @ wu
    m1 = np.mean(np.abs(a), axis=1, keepdims=True)
    hr = np.maximum(a - m1, 0.0) * f64(us)
    hid = hr.T
    hidq = mxq(hid, 0, "e5m2")
    p = wbu.T @ hidq
    pp = np.zeros((N, C))
    pp[:, idx3] = p
    y = pp + 0.5 * f64(old)
    words, scales = planes(y)
    return y, words, scales

@@ -1,0 +1,263 @@
+from contextlib import ExitStack
+
+import concourse.mybir as mybir
+from concourse.masks import make_identity
+
+K, T, J, S, R, N, C = 512, 512, 256, 512, 512, 512, 1024
+FLOPS = 2 * J * K * R + 2 * J * R * N
+
+F32 = mybir.dt.float32
+BF16 = mybir.dt.bfloat16
+I32 = mybir.dt.int32
+U32 = mybir.dt.uint32
+U16 = mybir.dt.uint16
+U8 = mybir.dt.uint8
+E4M3 = mybir.dt.float8_e4m3fn_x4
+E5M2 = mybir.dt.float8_e5m2_x4
+E2M1 = mybir.dt.float4_e2m1fn_x4
+ALU = mybir.AluOpType
+ACT = mybir.ActivationFunctionType
+
+P = 128
+PACK = 4
+HALF = J // 2
+LIST_COLS = HALF // 16
+CHUNK = 256
+CHUNKS = C // CHUNK
+
+
+def tile_list_rows_entryproducts_abovemean_scattered_pl_kernel(
+    tc, xa, xb, fk, w_words, w_scales, us, wb_words, wb_scales, old, offs, offs2, offs3, out_0, out_1, out_2
+):
+    nc = tc.nc
+    with ExitStack() as ctx:
+        keep = ctx.enter_context(tc.tile_pool(name="keep", bufs=1))
+        psum = ctx.enter_context(tc.psum_pool(name="psum", bufs=1))
+
+        def tiles(name, count, shape, dtype):
+            return [keep.tile(shape, dtype, name="%s%d" % (name, i), align_bytes=64) for i in range(count)]
+
+        list_a = keep.tile([P, J // 16], U16, name="list_a")
+        list_b = keep.tile([P, J // 16], U16, name="list_b")
+        list_c = keep.tile([P, J // 16], U16, name="list_c")
+        fk_sb = keep.tile([P, PACK], F32, name="fk_sb")
+        us_sb = keep.tile([P, 1, PACK], F32, name="us_sb")
+        xa_sb = tiles("xa", PACK, [P, T], F32)
+        xb_sb = tiles("xb", PACK, [P, S], F32)
+        page = tiles("page", PACK, [P, C], F32)
+        w_sb = keep.tile([P, R], U32, name="w_sb", align_bytes=64)
+        ws_sb = keep.tile([P, R], U8, name="ws_sb", align_bytes=64)
+        wb_raw = keep.tile([P, 2 * N], U8, name="wb_raw", align_bytes=64)
+        wbs_raw = keep.tile([P, N], U8, name="wbs_raw", align_bytes=64)
+        wb_sb = keep.tile([P, 2 * N], U8, name="wb_sb", align_bytes=64)
+        ident = keep.tile([P, P], F32, name="ident")
+
+        nc.gpsimd.memset(ws_sb[:].bitcast(I32), 0)
+        nc.gpsimd.memset(wbs_raw[:].bitcast(I32), 0)
+        for t in range(PACK):
+            nc.vector.memset(page[t][:], 0.0)
+
+        def load_scale_rows(queue, dst, src):
+            for q in range(4):
+                queue.dma_start(
+                    out=dst[32 * q : 32 * q + 4, :].bitcast(I32), in_=src[0, 4 * q : 4 * q + 4, :].bitcast(I32)
+                )
+
+        xa_rows = xa.rearrange("(p t) c -> p t c", t=PACK)
+        xb_rows = xb.rearrange("(p t) c -> p t c", t=PACK)
+        old_rows = old.rearrange("(p t) c -> p t c", t=PACK)
+        out_rows = out_0.rearrange("(p t) c -> p t c", t=PACK)
+        nc.sync.dma_start(list_b[:], offs2)
+        nc.sync.dma_start(list_a[:], offs)
+        nc.sync.dma_start(out=fk_sb[:], in_=fk.rearrange("(p t) o -> p (t o)", t=PACK))
+        for t in range(PACK):
+            nc.sync.dma_start(out=xb_sb[t][:], in_=xb_rows[:, t, :])
+            nc.sync.dma_start(out=xa_sb[t][:], in_=xa_rows[:, t, :])
+        nc.sync.dma_start(out=w_sb[:].bitcast(I32), in_=w_words[0].rearrange("p n t -> p (n t)").bitcast(I32))
+        load_scale_rows(nc.sync, ws_sb, w_scales)
+        nc.sync.dma_start(out=wb_raw[:].bitcast(I32), in_=wb_words[0].bitcast(I32))
+        load_scale_rows(nc.gpsimd, wbs_raw, wb_scales)
+        nc.gpsimd.dma_start(out=us_sb[:, 0, :], in_=us.rearrange("o (p t) -> (o p) t", t=PACK))
+        nc.sync.dma_start(list_c[:], offs3)
+        make_identity(nc, ident[:])
+
+        def half_list(lst, h):
+            return lst[:, h * LIST_COLS : (h + 1) * LIST_COLS]
+
+        b_pick = [keep.tile([P, J], F32, name="b_pick%d" % t, tag="pick%d" % t) for t in range(PACK)]
+        b_scaled = [keep.tile([P, J], F32, name="b_scaled%d" % t, tag="stage%d" % t) for t in range(PACK)]
+        u32 = keep.tile([P, PACK, J], F32, name="u32")
+        u_codes = tiles("u_codes", 2, [P, HALF], U32)
+        u_scales = [keep.tile([P, HALF], U8, name="u_scales%d" % h, tag="scales%d" % h, align_bytes=64) for h in range(2)]
+
+        def interleave(engine_copy, dst, src):
+            engine_copy(
+                out=dst.rearrange("p (c i t) -> p c t i", i=4, t=PACK),
+                in_=src.rearrange("p t (c i) -> p c t i", i=4),
+            )
+
+        def entries(lst, slots):
+            return lst[:, slots.start // 16 : slots.stop // 16]
+
+        def pick_b(t, slots):
+            nc.scalar.activation(out=b_pick[t][:, slots], in_=xb_sb[t][:].indirect(entries(list_b, slots)), func=ACT.Copy)
+            nc.scalar.activation(
+                out=b_scaled[t][:, slots], in_=b_pick[t][:, slots], func=ACT.Copy, scale=fk_sb[:, t : t + 1]
+            )
+
+        def pick_a(t, slots):
+            nc.vector.tensor_tensor(
+                u32[:, t, slots], xa_sb[t][:].indirect(entries(list_a, slots)), b_scaled[t][:, slots], ALU.mult
+            )
+
+        def quant_u(h):
+            u16 = keep.tile([P, HALF * PACK], BF16, name="u16", align_bytes=64)
+            interleave(nc.vector.tensor_copy, u16[:], u32[:, :, halves[h]])
+            nc.vector.quantize_mx(out=u_codes[h][:].bitcast(E4M3), scales=u_scales[h][:], in_=u16[:])
+
+        halves = [slice(0, HALF), slice(HALF, J)]
+        for t in range(PACK - 1):
+            pick_b(t, slice(0, J))
+            pick_a(t, slice(0, J))
+        for h in range(2):
+            pick_b(PACK - 1, halves[h])
+        for h in range(2):
+            pick_a(PACK - 1, halves[h])
+            quant_u(h)
+
+        old_sb = [keep.tile([P, C], F32, name="old%d" % t, tag="stage%d" % t) for t in range(PACK)]
+        for t in range(PACK):
+            nc.sync.dma_start(out=old_sb[t][:], in_=old_rows[:, t, :])
+
+        nc.scalar.copy(
+            out=wb_sb[:].bitcast(U16).rearrange("p (t q) -> p t q", t=PACK),
+            in_=wb_raw[:].bitcast(U16).rearrange("p (q t) -> p t q", t=PACK),
+        )
+
+        a_ps = [psum.tile([P, R], F32, name="a_ps%d" % h) for h in range(2)]
+        h_ps = [psum.tile([P, PACK, HALF], F32, name="h_ps%d" % h) for h in range(2)]
+        p_ps = [[psum.tile([P, 2, HALF], F32, name="p_ps%d%d" % (h, pair)) for pair in range(2)] for h in range(2)]
+        mags = tiles("mags", 2, [P, R], BF16)
+        mean = tiles("mean", 2, [P, 1], F32)
+        above = tiles("above", 2, [P, PACK, P], F32)
+        h_codes = tiles("h_codes", 2, [P, HALF], U32)
+        h_scales = tiles("h_scales", 2, [P, HALF], U8)
+        p_sb = tiles("p_sb", 2, [P, PACK, HALF], F32)
+
+        for h in range(2):
+            nc.tensor.matmul_mx(
+                out=a_ps[h][:],
+                lhsT=u_codes[h][:].bitcast(E4M3),
+                lhsT_scale=u_scales[h][:],
+                rhs=w_sb[:].bitcast(E4M3),
+                rhs_scale=ws_sb[:],
+                start=True,
+                stop=True,
+            )
+        wbs_sb = keep.tile([P, N], U8, name="wbs_sb", tag="scales0", align_bytes=64)
+        nc.vector.tensor_copy(
+            out=wbs_sb[:].rearrange("p (t q) -> p t q", t=PACK),
+            in_=wbs_raw[:].rearrange("p (q t) -> p t q", t=PACK),
+        )
+
+        for h in range(2):
+            nc.scalar.activation(
+                out=mags[h][:], in_=a_ps[h][:], func=ACT.Abs, scale=1.0 / R, accum_out=mean[h][:]
+            )
+        for h in range(2):
+            for pair in range(2):
+                nc.vector.tensor_scalar(
+                    out=above[h][:, 2 * pair : 2 * pair + 2, :],
+                    in0=a_ps[h][:].rearrange("p (q t) -> p t q", t=PACK)[:, 2 * pair : 2 * pair + 2, :],
+                    scalar1=mean[h][:],
+                    scalar2=0.0,
+                    op0=ALU.subtract,
+                    op1=ALU.max,
+                )
+                for t in (2 * pair, 2 * pair + 1):
+                    nc.tensor.transpose(h_ps[h][:, t, :], above[h][:, t, :], ident[:])
+
+        def second(h):
+            h16 = keep.tile([P, HALF, PACK], BF16, name="h16", align_bytes=64)
+            nc.vector.tensor_tensor(
+                h16[:],
+                h_ps[h][:].rearrange("p t j -> p j t"),
+                us_sb[:].to_broadcast([P, HALF, PACK]),
+                ALU.mult,
+            )
+            nc.vector.quantize_mx(
+                out=h_codes[h][:].bitcast(E5M2), scales=h_scales[h][:], in_=h16[:].rearrange("p j t -> p (j t)")
+            )
+            for t in range(PACK):
+                nc.tensor.matmul_mx(
+                    out=p_ps[h][t // 2][:, t % 2, :],
+                    lhsT=wb_sb[:, 2 * P * t : 2 * P * (t + 1)].bitcast(E2M1),
+                    lhsT_scale=wbs_sb[:, P * t : P * (t + 1)],
+                    rhs=h_codes[h][:].bitcast(E5M2),
+                    rhs_scale=h_scales[h][:],
+                    start=True,
+                    stop=True,
+                )
+
+        def put_scalar(t, h):
+            nc.scalar.activation(out=page[t][:].indirect(half_list(list_c, h)), in_=p_sb[h][:, t, :], func=ACT.Copy)
+
+        def put_vector(t, h):
+            nc.vector.tensor_copy(page[t][:].indirect(half_list(list_c, h)), p_sb[h][:, t, :])
+
+        second(0)
+        second(1)
+
+        def evacuate(engine_copy, h, pair):
+            engine_copy(out=p_sb[h][:, 2 * pair : 2 * pair + 2, :], in_=p_ps[h][pair][:])
+
+        evacuate(nc.scalar.copy, 0, 0)
+        put_scalar(1, 0)
+        put_vector(0, 0)
+        evacuate(nc.scalar.copy, 0, 1)
+        evacuate(nc.vector.tensor_copy, 1, 0)
+        put_vector(0, 1)
+        put_scalar(2, 0)
+        put_scalar(1, 1)
+        evacuate(nc.scalar.copy, 1, 1)
+        put_scalar(2, 1)
+        put_scalar(3, 0)
+        put_scalar(3, 1)
+
+        y = keep.tile([P, PACK, C], F32, name="y")
+        y16 = tiles("y16", CHUNKS, [P, CHUNK * PACK], BF16)
+        y_codes = tiles("y_codes", CHUNKS, [P, CHUNK], U32)
+        y_scales = keep.tile([P, C], U8, name="y_scales", align_bytes=64)
+        out_words = out_1[0].rearrange("p c t -> p (c t)").bitcast(I32)
+
+        def add_old(t, cols):
+            nc.vector.scalar_tensor_tensor(
+                out=y[:, t, cols], in0=old_sb[t][:, cols], scalar=0.5, in1=page[t][:, cols], op0=ALU.mult, op1=ALU.add
+            )
+
+        for t in range(PACK - 1):
+            add_old(t, slice(0, C))
+            nc.sync.dma_start(out=out_rows[:, t, :], in_=y[:, t, :])
+        for g in range(CHUNKS):
+            add_old(PACK - 1, slice(g * CHUNK, (g + 1) * CHUNK))
+        nc.sync.dma_start(out=out_rows[:, PACK - 1, :], in_=y[:, PACK - 1, :])
+
+        def round_chunk(g, engine_copy):
+            interleave(engine_copy, y16[g][:], y[:, :, g * CHUNK : (g + 1) * CHUNK])
+
+        def quant_chunk(g):
+            cols = slice(g * CHUNK, (g + 1) * CHUNK)
+            nc.vector.quantize_mx(out=y_codes[g][:].bitcast(E4M3), scales=y_scales[:, cols], in_=y16[g][:])
+            nc.sync.dma_start(out=out_words[:, cols], in_=y_codes[g][:].bitcast(I32))
+
+        round_chunk(0, nc.scalar.copy)
+        round_chunk(1, nc.scalar.copy)
+        round_chunk(2, nc.vector.tensor_copy)
+        round_chunk(3, nc.vector.tensor_copy)
+        for g in (0, 2, 3, 1):
+            quant_chunk(g)
+        for q in range(4):
+            queue = nc.sync if q % 2 == 0 else nc.scalar
+            queue.dma_start(
+                out=out_2[0, 4 * q : 4 * q + 4, :].bitcast(I32), in_=y_scales[32 * q : 32 * q + 4, :].bitcast(I32)
+            )

@@ -54,6 +54,9 @@ def tile_list_rows_entryproducts_abovemean_scattered_pl_kernel(
 
         nc.gpsimd.memset(ws_sb[:].bitcast(I32), 0)
         nc.gpsimd.memset(wbs_raw[:].bitcast(I32), 0)
+        warm = keep.tile([P, 2], F32, name="warm")
+        nc.vector.memset(warm[:, 0:1], 0.0)
+        nc.scalar.activation(out=warm[:, 1:2], in_=warm[:, 0:1], func=ACT.Abs)
         for t in range(PACK):
             nc.vector.memset(page[t][:], 0.0)
 

@@ -21,7 +21,7 @@ ACT = mybir.ActivationFunctionType
 P = 128
 PACK = 4
 HALF = J // 2
-LIST_COLS = HALF // 16
+QUARTER = J // 4
 CHUNK = 256
 CHUNKS = C // CHUNK
 
@@ -40,7 +40,7 @@ def tile_list_rows_entryproducts_abovemean_scattered_pl_kernel(
         list_a = keep.tile([P, J // 16], U16, name="list_a")
         list_b = keep.tile([P, J // 16], U16, name="list_b")
         list_c = keep.tile([P, J // 16], U16, name="list_c")
-        fk_sb = keep.tile([P, PACK], F32, name="fk_sb")
+        fk_sb = keep.tile([P, 1, PACK, 1], F32, name="fk_sb")
         us_sb = keep.tile([P, 1, PACK], F32, name="us_sb")
         xa_sb = tiles("xa", PACK, [P, T], F32)
         xb_sb = tiles("xb", PACK, [P, S], F32)
@@ -54,6 +54,7 @@ def tile_list_rows_entryproducts_abovemean_scattered_pl_kernel(
 
         nc.gpsimd.memset(ws_sb[:].bitcast(I32), 0)
         nc.gpsimd.memset(wbs_raw[:].bitcast(I32), 0)
+        make_identity(nc, ident[:])
         warm = keep.tile([P, 2], F32, name="warm")
         nc.vector.memset(warm[:, 0:1], 0.0)
         nc.scalar.activation(out=warm[:, 1:2], in_=warm[:, 0:1], func=ACT.Abs)
@@ -70,26 +71,23 @@ def tile_list_rows_entryproducts_abovemean_scattered_pl_kernel(
         xb_rows = xb.rearrange("(p t) c -> p t c", t=PACK)
         old_rows = old.rearrange("(p t) c -> p t c", t=PACK)
         out_rows = out_0.rearrange("(p t) c -> p t c", t=PACK)
-        nc.sync.dma_start(list_b[:], offs2)
-        nc.sync.dma_start(list_a[:], offs)
-        nc.sync.dma_start(out=fk_sb[:], in_=fk.rearrange("(p t) o -> p (t o)", t=PACK))
         for t in range(PACK):
             nc.sync.dma_start(out=xb_sb[t][:], in_=xb_rows[:, t, :])
+            if t == 0:
+                nc.sync.dma_start(list_b[:], offs2)
             nc.sync.dma_start(out=xa_sb[t][:], in_=xa_rows[:, t, :])
+            if t == 0:
+                nc.sync.dma_start(list_a[:], offs)
+        nc.sync.dma_start(out=wb_raw[:].bitcast(I32), in_=wb_words[0].bitcast(I32))
         nc.sync.dma_start(out=w_sb[:].bitcast(I32), in_=w_words[0].rearrange("p n t -> p (n t)").bitcast(I32))
         load_scale_rows(nc.sync, ws_sb, w_scales)
-        nc.sync.dma_start(out=wb_raw[:].bitcast(I32), in_=wb_words[0].bitcast(I32))
+        nc.gpsimd.dma_start(out=fk_sb[:, 0, :, 0], in_=fk.rearrange("(p t) o -> p (t o)", t=PACK))
         load_scale_rows(nc.gpsimd, wbs_raw, wb_scales)
-        nc.gpsimd.dma_start(out=us_sb[:, 0, :], in_=us.rearrange("o (p t) -> (o p) t", t=PACK))
+        nc.sync.dma_start(out=us_sb[:, 0, :], in_=us.rearrange("o (p t) -> (o p) t", t=PACK))
         nc.sync.dma_start(list_c[:], offs3)
-        make_identity(nc, ident[:])
-
-        def half_list(lst, h):
-            return lst[:, h * LIST_COLS : (h + 1) * LIST_COLS]
 
         b_pick = [keep.tile([P, J], F32, name="b_pick%d" % t, tag="pick%d" % t) for t in range(PACK)]
-        b_scaled = [keep.tile([P, J], F32, name="b_scaled%d" % t, tag="stage%d" % t) for t in range(PACK)]
-        u32 = keep.tile([P, PACK, J], F32, name="u32")
+        u32 = keep.tile([P, PACK, J], F32, name="u32", tag="products")
         u_codes = tiles("u_codes", 2, [P, HALF], U32)
         u_scales = [keep.tile([P, HALF], U8, name="u_scales%d" % h, tag="scales%d" % h, align_bytes=64) for h in range(2)]
 
@@ -104,48 +102,59 @@ def tile_list_rows_entryproducts_abovemean_scattered_pl_kernel(
 
         def pick_b(t, slots):
             nc.scalar.activation(out=b_pick[t][:, slots], in_=xb_sb[t][:].indirect(entries(list_b, slots)), func=ACT.Copy)
-            nc.scalar.activation(
-                out=b_scaled[t][:, slots], in_=b_pick[t][:, slots], func=ACT.Copy, scale=fk_sb[:, t : t + 1]
-            )
 
         def pick_a(t, slots):
             nc.vector.tensor_tensor(
-                u32[:, t, slots], xa_sb[t][:].indirect(entries(list_a, slots)), b_scaled[t][:, slots], ALU.mult
+                u32[:, t, slots], xa_sb[t][:].indirect(entries(list_a, slots)), b_pick[t][:, slots], ALU.mult
             )
 
+        u16 = tiles("u16", 4, [P, QUARTER * PACK], BF16)
+
         def quant_u(h):
-            u16 = keep.tile([P, HALF * PACK], BF16, name="u16", align_bytes=64)
-            interleave(nc.vector.tensor_copy, u16[:], u32[:, :, halves[h]])
-            nc.vector.quantize_mx(out=u_codes[h][:].bitcast(E4M3), scales=u_scales[h][:], in_=u16[:])
+            for g in range(2):
+                first = h * HALF + g * QUARTER
+                nc.vector.tensor_tensor(
+                    u16[2 * h + g][:].rearrange("p (c i t) -> p c t i", i=4, t=PACK),
+                    u32[:, :, first : first + QUARTER].rearrange("p t (c i) -> p c t i", i=4),
+                    fk_sb[:].to_broadcast([P, QUARTER // 4, PACK, 4]),
+                    ALU.mult,
+                )
+            for g in range(2):
+                cols = slice(g * QUARTER, (g + 1) * QUARTER)
+                nc.vector.quantize_mx(
+                    out=u_codes[h][:, cols].bitcast(E4M3), scales=u_scales[h][:, cols], in_=u16[2 * h + g][:]
+                )
 
         halves = [slice(0, HALF), slice(HALF, J)]
         for t in range(PACK - 1):
             pick_b(t, slice(0, J))
             pick_a(t, slice(0, J))
+        pick_b(PACK - 1, slice(0, J))
+        last = PACK - 1
+        pick_a(last, halves[0])
+        a_pick = keep.tile([P, HALF], F32, name="a_pick")
+        nc.scalar.activation(out=a_pick[:], in_=xa_sb[last][:].indirect(entries(list_a, halves[1])), func=ACT.Copy)
+        nc.vector.tensor_tensor(u32[:, last, halves[1]], a_pick[:], b_pick[last][:, halves[1]], ALU.mult)
         for h in range(2):
-            pick_b(PACK - 1, halves[h])
-        for h in range(2):
-            pick_a(PACK - 1, halves[h])
             quant_u(h)
 
-        old_sb = [keep.tile([P, C], F32, name="old%d" % t, tag="stage%d" % t) for t in range(PACK)]
-        for t in range(PACK):
-            nc.sync.dma_start(out=old_sb[t][:], in_=old_rows[:, t, :])
+        old_sb = [keep.tile([P, 2, C], F32, name="old%d" % i, tag=tag) for i, tag in enumerate(("pick3", "products"))]
+        for i in range(2):
+            nc.sync.dma_start(out=old_sb[i][:], in_=old_rows[:, 2 * i : 2 * i + 2, :])
 
         nc.scalar.copy(
             out=wb_sb[:].bitcast(U16).rearrange("p (t q) -> p t q", t=PACK),
             in_=wb_raw[:].bitcast(U16).rearrange("p (q t) -> p t q", t=PACK),
         )
 
-        a_ps = [psum.tile([P, R], F32, name="a_ps%d" % h) for h in range(2)]
+        a_ps = [psum.tile([P, R], F32, name="a_ps%d" % h, tag="a%d" % h) for h in range(2)]
         h_ps = [psum.tile([P, PACK, HALF], F32, name="h_ps%d" % h) for h in range(2)]
-        p_ps = [[psum.tile([P, 2, HALF], F32, name="p_ps%d%d" % (h, pair)) for pair in range(2)] for h in range(2)]
         mags = tiles("mags", 2, [P, R], BF16)
         mean = tiles("mean", 2, [P, 1], F32)
         above = tiles("above", 2, [P, PACK, P], F32)
         h_codes = tiles("h_codes", 2, [P, HALF], U32)
         h_scales = tiles("h_scales", 2, [P, HALF], U8)
-        p_sb = tiles("p_sb", 2, [P, PACK, HALF], F32)
+        p_sb = keep.tile([P, PACK, J], F32, name="p_sb")
 
         for h in range(2):
             nc.tensor.matmul_mx(
@@ -180,20 +189,31 @@ def tile_list_rows_entryproducts_abovemean_scattered_pl_kernel(
                 for t in (2 * pair, 2 * pair + 1):
                     nc.tensor.transpose(h_ps[h][:, t, :], above[h][:, t, :], ident[:])
 
+        p_early = [
+            [psum.tile([P, HALF], F32, name="p%d%d" % (h, t), tag="a0" if (h, t) == (1, 1) else "p%d%d" % (h, t)) for t in range(2)]
+            for h in range(2)
+        ]
+        p_late = psum.tile([P, 2, J], F32, name="p_late")
+        h16 = tiles("h16", 4, [P, QUARTER, PACK], BF16)
+
         def second(h):
-            h16 = keep.tile([P, HALF, PACK], BF16, name="h16", align_bytes=64)
-            nc.vector.tensor_tensor(
-                h16[:],
-                h_ps[h][:].rearrange("p t j -> p j t"),
-                us_sb[:].to_broadcast([P, HALF, PACK]),
-                ALU.mult,
-            )
-            nc.vector.quantize_mx(
-                out=h_codes[h][:].bitcast(E5M2), scales=h_scales[h][:], in_=h16[:].rearrange("p j t -> p (j t)")
-            )
-            for t in range(PACK):
+            for g in range(2):
+                nc.vector.tensor_tensor(
+                    h16[2 * h + g][:],
+                    h_ps[h][:, :, g * QUARTER : (g + 1) * QUARTER].rearrange("p t j -> p j t"),
+                    us_sb[:].to_broadcast([P, QUARTER, PACK]),
+                    ALU.mult,
+                )
+            for g in range(2):
+                cols = slice(g * QUARTER, (g + 1) * QUARTER)
+                nc.vector.quantize_mx(
+                    out=h_codes[h][:, cols].bitcast(E5M2),
+                    scales=h_scales[h][:, cols],
+                    in_=h16[2 * h + g][:].rearrange("p j t -> p (j t)"),
+                )
+            for t in ((1, 0, 2, 3), (0, 1, 2, 3))[h]:
                 nc.tensor.matmul_mx(
-                    out=p_ps[h][t // 2][:, t % 2, :],
+                    out=p_early[h][t][:] if t < 2 else p_late[:, t - 2, halves[h]],
                     lhsT=wb_sb[:, 2 * P * t : 2 * P * (t + 1)].bitcast(E2M1),
                     lhsT_scale=wbs_sb[:, P * t : P * (t + 1)],
                     rhs=h_codes[h][:].bitcast(E5M2),
@@ -202,30 +222,25 @@ def tile_list_rows_entryproducts_abovemean_scattered_pl_kernel(
                     stop=True,
                 )
 
-        def put_scalar(t, h):
-            nc.scalar.activation(out=page[t][:].indirect(half_list(list_c, h)), in_=p_sb[h][:, t, :], func=ACT.Copy)
+        def put_scalar(t, slots):
+            nc.scalar.activation(out=page[t][:].indirect(entries(list_c, slots)), in_=p_sb[:, t, slots], func=ACT.Copy)
 
-        def put_vector(t, h):
-            nc.vector.tensor_copy(page[t][:].indirect(half_list(list_c, h)), p_sb[h][:, t, :])
+        def put_vector(t, slots):
+            nc.vector.tensor_copy(page[t][:].indirect(entries(list_c, slots)), p_sb[:, t, slots])
 
         second(0)
         second(1)
 
-        def evacuate(engine_copy, h, pair):
-            engine_copy(out=p_sb[h][:, 2 * pair : 2 * pair + 2, :], in_=p_ps[h][pair][:])
-
-        evacuate(nc.scalar.copy, 0, 0)
-        put_scalar(1, 0)
-        put_vector(0, 0)
-        evacuate(nc.scalar.copy, 0, 1)
-        evacuate(nc.vector.tensor_copy, 1, 0)
-        put_vector(0, 1)
-        put_scalar(2, 0)
-        put_scalar(1, 1)
-        evacuate(nc.scalar.copy, 1, 1)
-        put_scalar(2, 1)
-        put_scalar(3, 0)
-        put_scalar(3, 1)
+        nc.scalar.copy(out=p_sb[:, 1, halves[0]], in_=p_early[0][1][:])
+        put_scalar(1, halves[0])
+        for h in range(2):
+            nc.vector.tensor_copy(out=p_sb[:, 0, halves[h]], in_=p_early[h][0][:])
+            put_vector(0, halves[h])
+        nc.scalar.copy(out=p_sb[:, 1, halves[1]], in_=p_early[1][1][:])
+        nc.scalar.copy(out=p_sb[:, 2:4, :], in_=p_late[:])
+        put_scalar(1, halves[1])
+        put_scalar(2, slice(0, J))
+        put_scalar(3, slice(0, J))
 
         y = keep.tile([P, PACK, C], F32, name="y")
         y16 = tiles("y16", CHUNKS, [P, CHUNK * PACK], BF16)
@@ -235,10 +250,13 @@ def tile_list_rows_entryproducts_abovemean_scattered_pl_kernel(
 
         def add_old(t, cols):
             nc.vector.scalar_tensor_tensor(
-                out=y[:, t, cols], in0=old_sb[t][:, cols], scalar=0.5, in1=page[t][:, cols], op0=ALU.mult, op1=ALU.add
+                out=y[:, t, cols], in0=old_sb[t // 2][:, t % 2, cols], scalar=0.5, in1=page[t][:, cols], op0=ALU.mult, op1=ALU.add
             )
 
-        for t in range(PACK - 1):
+        for cols in (slice(0, C // 2), slice(C // 2, C)):
+            add_old(0, cols)
+            nc.sync.dma_start(out=out_rows[:, 0, cols], in_=y[:, 0, cols])
+        for t in range(1, PACK - 1):
             add_old(t, slice(0, C))
             nc.sync.dma_start(out=out_rows[:, t, :], in_=y[:, t, :])
         for g in range(CHUNKS):

@@ -20,10 +20,16 @@ ACT = mybir.ActivationFunctionType
 
 P = 128
 PACK = 4
+LAST = PACK - 1
 HALF = J // 2
 QUARTER = J // 4
+RUN = 4
 CHUNK = 256
 CHUNKS = C // CHUNK
+QUADRANTS = 4
+
+ALL_SLOTS = slice(0, J)
+HALVES = (slice(0, HALF), slice(HALF, J))
 
 
 def tile_list_rows_entryproducts_abovemean_scattered_pl_kernel(
@@ -36,6 +42,12 @@ def tile_list_rows_entryproducts_abovemean_scattered_pl_kernel(
 
         def tiles(name, count, shape, dtype):
             return [keep.tile(shape, dtype, name="%s%d" % (name, i), align_bytes=64) for i in range(count)]
+
+        def entries(list_tile, slots):
+            return list_tile[:, slots.start // 16 : slots.stop // 16]
+
+        def scale_partitions(q):
+            return slice(32 * q, 32 * q + 4)
 
         list_a = keep.tile([P, J // 16], U16, name="list_a")
         list_b = keep.tile([P, J // 16], U16, name="list_b")
@@ -62,22 +74,22 @@ def tile_list_rows_entryproducts_abovemean_scattered_pl_kernel(
             nc.vector.memset(page[t][:], 0.0)
 
         def load_scale_rows(queue, dst, src):
-            for q in range(4):
+            for q in range(QUADRANTS):
                 queue.dma_start(
-                    out=dst[32 * q : 32 * q + 4, :].bitcast(I32), in_=src[0, 4 * q : 4 * q + 4, :].bitcast(I32)
+                    out=dst[scale_partitions(q), :].bitcast(I32), in_=src[0, 4 * q : 4 * q + 4, :].bitcast(I32)
                 )
 
         xa_rows = xa.rearrange("(p t) c -> p t c", t=PACK)
         xb_rows = xb.rearrange("(p t) c -> p t c", t=PACK)
         old_rows = old.rearrange("(p t) c -> p t c", t=PACK)
         out_rows = out_0.rearrange("(p t) c -> p t c", t=PACK)
-        for t in range(PACK):
+        nc.sync.dma_start(out=xb_sb[0][:], in_=xb_rows[:, 0, :])
+        nc.sync.dma_start(list_b[:], offs2)
+        nc.sync.dma_start(out=xa_sb[0][:], in_=xa_rows[:, 0, :])
+        nc.sync.dma_start(list_a[:], offs)
+        for t in range(1, PACK):
             nc.sync.dma_start(out=xb_sb[t][:], in_=xb_rows[:, t, :])
-            if t == 0:
-                nc.sync.dma_start(list_b[:], offs2)
             nc.sync.dma_start(out=xa_sb[t][:], in_=xa_rows[:, t, :])
-            if t == 0:
-                nc.sync.dma_start(list_a[:], offs)
         nc.sync.dma_start(out=wb_raw[:].bitcast(I32), in_=wb_words[0].bitcast(I32))
         nc.sync.dma_start(out=w_sb[:].bitcast(I32), in_=w_words[0].rearrange("p n t -> p (n t)").bitcast(I32))
         load_scale_rows(nc.sync, ws_sb, w_scales)
@@ -87,36 +99,28 @@ def tile_list_rows_entryproducts_abovemean_scattered_pl_kernel(
         nc.sync.dma_start(list_c[:], offs3)
 
         b_pick = [keep.tile([P, J], F32, name="b_pick%d" % t, tag="pick%d" % t) for t in range(PACK)]
-        u32 = keep.tile([P, PACK, J], F32, name="u32", tag="products")
+        ab = keep.tile([P, PACK, J], F32, name="ab", tag="products")
         u_codes = tiles("u_codes", 2, [P, HALF], U32)
-        u_scales = [keep.tile([P, HALF], U8, name="u_scales%d" % h, tag="scales%d" % h, align_bytes=64) for h in range(2)]
-
-        def interleave(engine_copy, dst, src):
-            engine_copy(
-                out=dst.rearrange("p (c i t) -> p c t i", i=4, t=PACK),
-                in_=src.rearrange("p t (c i) -> p c t i", i=4),
-            )
-
-        def entries(lst, slots):
-            return lst[:, slots.start // 16 : slots.stop // 16]
-
-        def pick_b(t, slots):
-            nc.scalar.activation(out=b_pick[t][:, slots], in_=xb_sb[t][:].indirect(entries(list_b, slots)), func=ACT.Copy)
-
-        def pick_a(t, slots):
-            nc.vector.tensor_tensor(
-                u32[:, t, slots], xa_sb[t][:].indirect(entries(list_a, slots)), b_pick[t][:, slots], ALU.mult
-            )
-
+        u_scales = [
+            keep.tile([P, HALF], U8, name="u_scales%d" % h, tag="scales%d" % h, align_bytes=64) for h in range(2)
+        ]
         u16 = tiles("u16", 4, [P, QUARTER * PACK], BF16)
 
-        def quant_u(h):
+        def pick_b(t):
+            nc.scalar.activation(out=b_pick[t][:], in_=xb_sb[t][:].indirect(list_b[:]), func=ACT.Copy)
+
+        def pick_a_times_b(t, slots):
+            nc.vector.tensor_tensor(
+                ab[:, t, slots], xa_sb[t][:].indirect(entries(list_a, slots)), b_pick[t][:, slots], ALU.mult
+            )
+
+        def quantise_u(h):
             for g in range(2):
                 first = h * HALF + g * QUARTER
                 nc.vector.tensor_tensor(
-                    u16[2 * h + g][:].rearrange("p (c i t) -> p c t i", i=4, t=PACK),
-                    u32[:, :, first : first + QUARTER].rearrange("p t (c i) -> p c t i", i=4),
-                    fk_sb[:].to_broadcast([P, QUARTER // 4, PACK, 4]),
+                    u16[2 * h + g][:].rearrange("p (c i t) -> p c t i", i=RUN, t=PACK),
+                    ab[:, :, first : first + QUARTER].rearrange("p t (c i) -> p c t i", i=RUN),
+                    fk_sb[:].to_broadcast([P, QUARTER // RUN, PACK, RUN]),
                     ALU.mult,
                 )
             for g in range(2):
@@ -125,20 +129,20 @@ def tile_list_rows_entryproducts_abovemean_scattered_pl_kernel(
                     out=u_codes[h][:, cols].bitcast(E4M3), scales=u_scales[h][:, cols], in_=u16[2 * h + g][:]
                 )
 
-        halves = [slice(0, HALF), slice(HALF, J)]
-        for t in range(PACK - 1):
-            pick_b(t, slice(0, J))
-            pick_a(t, slice(0, J))
-        pick_b(PACK - 1, slice(0, J))
-        last = PACK - 1
-        pick_a(last, halves[0])
+        for t in range(LAST):
+            pick_b(t)
+            pick_a_times_b(t, ALL_SLOTS)
+        pick_b(LAST)
+        pick_a_times_b(LAST, HALVES[0])
         a_pick = keep.tile([P, HALF], F32, name="a_pick")
-        nc.scalar.activation(out=a_pick[:], in_=xa_sb[last][:].indirect(entries(list_a, halves[1])), func=ACT.Copy)
-        nc.vector.tensor_tensor(u32[:, last, halves[1]], a_pick[:], b_pick[last][:, halves[1]], ALU.mult)
+        nc.scalar.activation(out=a_pick[:], in_=xa_sb[LAST][:].indirect(entries(list_a, HALVES[1])), func=ACT.Copy)
+        nc.vector.tensor_tensor(ab[:, LAST, HALVES[1]], a_pick[:], b_pick[LAST][:, HALVES[1]], ALU.mult)
         for h in range(2):
-            quant_u(h)
+            quantise_u(h)
 
-        old_sb = [keep.tile([P, 2, C], F32, name="old%d" % i, tag=tag) for i, tag in enumerate(("pick3", "products"))]
+        old_sb = [
+            keep.tile([P, 2, C], F32, name="old%d" % i, tag=tag) for i, tag in enumerate(("pick%d" % LAST, "products"))
+        ]
         for i in range(2):
             nc.sync.dma_start(out=old_sb[i][:], in_=old_rows[:, 2 * i : 2 * i + 2, :])
 
@@ -173,30 +177,28 @@ def tile_list_rows_entryproducts_abovemean_scattered_pl_kernel(
         )
 
         for h in range(2):
-            nc.scalar.activation(
-                out=mags[h][:], in_=a_ps[h][:], func=ACT.Abs, scale=1.0 / R, accum_out=mean[h][:]
-            )
+            nc.scalar.activation(out=mags[h][:], in_=a_ps[h][:], func=ACT.Abs, scale=1.0 / R, accum_out=mean[h][:])
         for h in range(2):
-            for pair in range(2):
+            for first in (0, 2):
                 nc.vector.tensor_scalar(
-                    out=above[h][:, 2 * pair : 2 * pair + 2, :],
-                    in0=a_ps[h][:].rearrange("p (q t) -> p t q", t=PACK)[:, 2 * pair : 2 * pair + 2, :],
+                    out=above[h][:, first : first + 2, :],
+                    in0=a_ps[h][:].rearrange("p (q t) -> p t q", t=PACK)[:, first : first + 2, :],
                     scalar1=mean[h][:],
                     scalar2=0.0,
                     op0=ALU.subtract,
                     op1=ALU.max,
                 )
-                for t in (2 * pair, 2 * pair + 1):
+                for t in (first, first + 1):
                     nc.tensor.transpose(h_ps[h][:, t, :], above[h][:, t, :], ident[:])
 
+        early_tags = (("p00", "p01"), ("p10", "a0"))
         p_early = [
-            [psum.tile([P, HALF], F32, name="p%d%d" % (h, t), tag="a0" if (h, t) == (1, 1) else "p%d%d" % (h, t)) for t in range(2)]
-            for h in range(2)
+            [psum.tile([P, HALF], F32, name="p%d%d" % (h, t), tag=early_tags[h][t]) for t in range(2)] for h in range(2)
         ]
         p_late = psum.tile([P, 2, J], F32, name="p_late")
         h16 = tiles("h16", 4, [P, QUARTER, PACK], BF16)
 
-        def second(h):
+        def quantise_hid(h):
             for g in range(2):
                 nc.vector.tensor_tensor(
                     h16[2 * h + g][:],
@@ -211,74 +213,85 @@ def tile_list_rows_entryproducts_abovemean_scattered_pl_kernel(
                     scales=h_scales[h][:, cols],
                     in_=h16[2 * h + g][:].rearrange("p j t -> p (j t)"),
                 )
-            for t in ((1, 0, 2, 3), (0, 1, 2, 3))[h]:
-                nc.tensor.matmul_mx(
-                    out=p_early[h][t][:] if t < 2 else p_late[:, t - 2, halves[h]],
-                    lhsT=wb_sb[:, 2 * P * t : 2 * P * (t + 1)].bitcast(E2M1),
-                    lhsT_scale=wbs_sb[:, P * t : P * (t + 1)],
-                    rhs=h_codes[h][:].bitcast(E5M2),
-                    rhs_scale=h_scales[h][:],
-                    start=True,
-                    stop=True,
-                )
 
-        def put_scalar(t, slots):
+        def second_product(h, t):
+            nc.tensor.matmul_mx(
+                out=p_early[h][t][:] if t < 2 else p_late[:, t - 2, HALVES[h]],
+                lhsT=wb_sb[:, 2 * P * t : 2 * P * (t + 1)].bitcast(E2M1),
+                lhsT_scale=wbs_sb[:, P * t : P * (t + 1)],
+                rhs=h_codes[h][:].bitcast(E5M2),
+                rhs_scale=h_scales[h][:],
+                start=True,
+                stop=True,
+            )
+
+        def put_on_scalar(t, slots):
             nc.scalar.activation(out=page[t][:].indirect(entries(list_c, slots)), in_=p_sb[:, t, slots], func=ACT.Copy)
 
-        def put_vector(t, slots):
+        def put_on_vector(t, slots):
             nc.vector.tensor_copy(page[t][:].indirect(entries(list_c, slots)), p_sb[:, t, slots])
 
-        second(0)
-        second(1)
+        for h, planes in enumerate(((1, 0, 2, 3), (0, 1, 2, 3))):
+            quantise_hid(h)
+            for t in planes:
+                second_product(h, t)
 
-        nc.scalar.copy(out=p_sb[:, 1, halves[0]], in_=p_early[0][1][:])
-        put_scalar(1, halves[0])
+        nc.scalar.copy(out=p_sb[:, 1, HALVES[0]], in_=p_early[0][1][:])
+        put_on_scalar(1, HALVES[0])
         for h in range(2):
-            nc.vector.tensor_copy(out=p_sb[:, 0, halves[h]], in_=p_early[h][0][:])
-            put_vector(0, halves[h])
-        nc.scalar.copy(out=p_sb[:, 1, halves[1]], in_=p_early[1][1][:])
-        nc.scalar.copy(out=p_sb[:, 2:4, :], in_=p_late[:])
-        put_scalar(1, halves[1])
-        put_scalar(2, slice(0, J))
-        put_scalar(3, slice(0, J))
+            nc.vector.tensor_copy(out=p_sb[:, 0, HALVES[h]], in_=p_early[h][0][:])
+            put_on_vector(0, HALVES[h])
+        nc.scalar.copy(out=p_sb[:, 1, HALVES[1]], in_=p_early[1][1][:])
+        nc.scalar.copy(out=p_sb[:, 2:PACK, :], in_=p_late[:])
+        put_on_scalar(1, HALVES[1])
+        for t in (2, 3):
+            put_on_scalar(t, ALL_SLOTS)
 
         y = keep.tile([P, PACK, C], F32, name="y")
         y16 = tiles("y16", CHUNKS, [P, CHUNK * PACK], BF16)
-        y_codes = tiles("y_codes", CHUNKS, [P, CHUNK], U32)
+        y_codes = keep.tile([P, C], U32, name="y_codes", align_bytes=64)
         y_scales = keep.tile([P, C], U8, name="y_scales", align_bytes=64)
         out_words = out_1[0].rearrange("p c t -> p (c t)").bitcast(I32)
 
+        def chunk_cols(first, count):
+            return slice(first * CHUNK, (first + count) * CHUNK)
+
         def add_old(t, cols):
             nc.vector.scalar_tensor_tensor(
-                out=y[:, t, cols], in0=old_sb[t // 2][:, t % 2, cols], scalar=0.5, in1=page[t][:, cols], op0=ALU.mult, op1=ALU.add
+                out=y[:, t, cols],
+                in0=old_sb[t // 2][:, t % 2, cols],
+                scalar=0.5,
+                in1=page[t][:, cols],
+                op0=ALU.mult,
+                op1=ALU.add,
             )
 
-        for cols in (slice(0, C // 2), slice(C // 2, C)):
+        for first in (0, CHUNKS // 2):
+            cols = chunk_cols(first, CHUNKS // 2)
             add_old(0, cols)
             nc.sync.dma_start(out=out_rows[:, 0, cols], in_=y[:, 0, cols])
-        for t in range(1, PACK - 1):
-            add_old(t, slice(0, C))
+        for t in range(1, LAST):
+            add_old(t, chunk_cols(0, CHUNKS))
             nc.sync.dma_start(out=out_rows[:, t, :], in_=y[:, t, :])
         for g in range(CHUNKS):
-            add_old(PACK - 1, slice(g * CHUNK, (g + 1) * CHUNK))
-        nc.sync.dma_start(out=out_rows[:, PACK - 1, :], in_=y[:, PACK - 1, :])
+            add_old(LAST, chunk_cols(g, 1))
+        nc.sync.dma_start(out=out_rows[:, LAST, :], in_=y[:, LAST, :])
 
-        def round_chunk(g, engine_copy):
-            interleave(engine_copy, y16[g][:], y[:, :, g * CHUNK : (g + 1) * CHUNK])
+        for g in range(CHUNKS):
+            round_and_interleave = nc.scalar.copy if g in (0, CHUNKS - 1) else nc.vector.tensor_copy
+            round_and_interleave(
+                out=y16[g][:].rearrange("p (c i t) -> p c t i", i=RUN, t=PACK),
+                in_=y[:, :, chunk_cols(g, 1)].rearrange("p t (c i) -> p c t i", i=RUN),
+            )
 
-        def quant_chunk(g):
-            cols = slice(g * CHUNK, (g + 1) * CHUNK)
-            nc.vector.quantize_mx(out=y_codes[g][:].bitcast(E4M3), scales=y_scales[:, cols], in_=y16[g][:])
-            nc.sync.dma_start(out=out_words[:, cols], in_=y_codes[g][:].bitcast(I32))
-
-        round_chunk(0, nc.scalar.copy)
-        round_chunk(1, nc.scalar.copy)
-        round_chunk(2, nc.vector.tensor_copy)
-        round_chunk(3, nc.vector.tensor_copy)
-        for g in (0, 2, 3, 1):
-            quant_chunk(g)
-        for q in range(4):
+        for first, count in ((0, 2), (2, 1), (3, 1)):
+            for g in range(first, first + count):
+                cols = chunk_cols(g, 1)
+                nc.vector.quantize_mx(out=y_codes[:, cols].bitcast(E4M3), scales=y_scales[:, cols], in_=y16[g][:])
+            cols = chunk_cols(first, count)
+            nc.sync.dma_start(out=out_words[:, cols], in_=y_codes[:, cols].bitcast(I32))
+        for q in range(QUADRANTS):
             queue = nc.sync if q % 2 == 0 else nc.scalar
             queue.dma_start(
-                out=out_2[0, 4 * q : 4 * q + 4, :].bitcast(I32), in_=y_scales[32 * q : 32 * q + 4, :].bitcast(I32)
+                out=out_2[0, 4 * q : 4 * q + 4, :].bitcast(I32), in_=y_scales[scale_partitions(q), :].bitcast(I32)
             )

from contextlib import ExitStack

import concourse.mybir as mybir
from concourse.masks import make_identity

K, T, J, S, R, N, C = 512, 512, 256, 512, 512, 512, 1024
FLOPS = 2 * J * K * R + 2 * J * R * N

F32 = mybir.dt.float32
BF16 = mybir.dt.bfloat16
I32 = mybir.dt.int32
U32 = mybir.dt.uint32
U16 = mybir.dt.uint16
U8 = mybir.dt.uint8
E4M3 = mybir.dt.float8_e4m3fn_x4
E5M2 = mybir.dt.float8_e5m2_x4
E2M1 = mybir.dt.float4_e2m1fn_x4
ALU = mybir.AluOpType
ACT = mybir.ActivationFunctionType

P = 128
PACK = 4
LAST = PACK - 1
HALF = J // 2
QUARTER = J // 4
RUN = 4
CHUNK = 256
CHUNKS = C // CHUNK
QUADRANTS = 4

ALL_SLOTS = slice(0, J)
HALVES = (slice(0, HALF), slice(HALF, J))


def tile_list_rows_entryproducts_abovemean_scattered_pl_kernel(
    tc, xa, xb, fk, w_words, w_scales, us, wb_words, wb_scales, old, offs, offs2, offs3, out_0, out_1, out_2
):
    nc = tc.nc
    with ExitStack() as ctx:
        keep = ctx.enter_context(tc.tile_pool(name="keep", bufs=1))
        psum = ctx.enter_context(tc.psum_pool(name="psum", bufs=1))

        def tiles(name, count, shape, dtype):
            return [keep.tile(shape, dtype, name="%s%d" % (name, i), align_bytes=64) for i in range(count)]

        def entries(list_tile, slots):
            return list_tile[:, slots.start // 16 : slots.stop // 16]

        def scale_partitions(q):
            return slice(32 * q, 32 * q + 4)

        list_a = keep.tile([P, J // 16], U16, name="list_a")
        list_b = keep.tile([P, J // 16], U16, name="list_b")
        list_c = keep.tile([P, J // 16], U16, name="list_c")
        fk_sb = keep.tile([P, 1, PACK, 1], F32, name="fk_sb")
        us_sb = keep.tile([P, 1, PACK], F32, name="us_sb")
        xa_sb = tiles("xa", PACK, [P, T], F32)
        xb_sb = tiles("xb", PACK, [P, S], F32)
        page = tiles("page", PACK, [P, C], F32)
        w_sb = keep.tile([P, R], U32, name="w_sb", align_bytes=64)
        ws_sb = keep.tile([P, R], U8, name="ws_sb", align_bytes=64)
        wb_raw = keep.tile([P, 2 * N], U8, name="wb_raw", align_bytes=64)
        wbs_raw = keep.tile([P, N], U8, name="wbs_raw", align_bytes=64)
        wb_sb = keep.tile([P, 2 * N], U8, name="wb_sb", align_bytes=64)
        ident = keep.tile([P, P], F32, name="ident")

        nc.gpsimd.memset(ws_sb[:].bitcast(I32), 0)
        nc.gpsimd.memset(wbs_raw[:].bitcast(I32), 0)
        make_identity(nc, ident[:])
        warm = keep.tile([P, 2], F32, name="warm")
        nc.vector.memset(warm[:, 0:1], 0.0)
        nc.scalar.activation(out=warm[:, 1:2], in_=warm[:, 0:1], func=ACT.Abs)
        for t in range(PACK):
            nc.vector.memset(page[t][:], 0.0)

        def load_scale_rows(queue, dst, src):
            for q in range(QUADRANTS):
                queue.dma_start(
                    out=dst[scale_partitions(q), :].bitcast(I32), in_=src[0, 4 * q : 4 * q + 4, :].bitcast(I32)
                )

        xa_rows = xa.rearrange("(p t) c -> p t c", t=PACK)
        xb_rows = xb.rearrange("(p t) c -> p t c", t=PACK)
        old_rows = old.rearrange("(p t) c -> p t c", t=PACK)
        out_rows = out_0.rearrange("(p t) c -> p t c", t=PACK)
        nc.sync.dma_start(out=xb_sb[0][:], in_=xb_rows[:, 0, :])
        nc.sync.dma_start(list_b[:], offs2)
        nc.sync.dma_start(out=xa_sb[0][:], in_=xa_rows[:, 0, :])
        nc.sync.dma_start(list_a[:], offs)
        for t in range(1, PACK):
            nc.sync.dma_start(out=xb_sb[t][:], in_=xb_rows[:, t, :])
            nc.sync.dma_start(out=xa_sb[t][:], in_=xa_rows[:, t, :])
        nc.sync.dma_start(out=wb_raw[:].bitcast(I32), in_=wb_words[0].bitcast(I32))
        nc.sync.dma_start(out=w_sb[:].bitcast(I32), in_=w_words[0].rearrange("p n t -> p (n t)").bitcast(I32))
        load_scale_rows(nc.sync, ws_sb, w_scales)
        nc.gpsimd.dma_start(out=fk_sb[:, 0, :, 0], in_=fk.rearrange("(p t) o -> p (t o)", t=PACK))
        load_scale_rows(nc.gpsimd, wbs_raw, wb_scales)
        nc.sync.dma_start(out=us_sb[:, 0, :], in_=us.rearrange("o (p t) -> (o p) t", t=PACK))
        nc.sync.dma_start(list_c[:], offs3)

        b_pick = [keep.tile([P, J], F32, name="b_pick%d" % t, tag="pick%d" % t) for t in range(PACK)]
        ab = keep.tile([P, PACK, J], F32, name="ab", tag="products")
        u_codes = tiles("u_codes", 2, [P, HALF], U32)
        u_scales = [
            keep.tile([P, HALF], U8, name="u_scales%d" % h, tag="scales%d" % h, align_bytes=64) for h in range(2)
        ]
        u16 = tiles("u16", 4, [P, QUARTER * PACK], BF16)

        def pick_b(t):
            nc.scalar.activation(out=b_pick[t][:], in_=xb_sb[t][:].indirect(list_b[:]), func=ACT.Copy)

        def pick_a_times_b(t, slots):
            nc.vector.tensor_tensor(
                ab[:, t, slots], xa_sb[t][:].indirect(entries(list_a, slots)), b_pick[t][:, slots], ALU.mult
            )

        def quantise_u(h):
            for g in range(2):
                first = h * HALF + g * QUARTER
                nc.vector.tensor_tensor(
                    u16[2 * h + g][:].rearrange("p (c i t) -> p c t i", i=RUN, t=PACK),
                    ab[:, :, first : first + QUARTER].rearrange("p t (c i) -> p c t i", i=RUN),
                    fk_sb[:].to_broadcast([P, QUARTER // RUN, PACK, RUN]),
                    ALU.mult,
                )
            for g in range(2):
                cols = slice(g * QUARTER, (g + 1) * QUARTER)
                nc.vector.quantize_mx(
                    out=u_codes[h][:, cols].bitcast(E4M3), scales=u_scales[h][:, cols], in_=u16[2 * h + g][:]
                )

        for t in range(LAST):
            pick_b(t)
            pick_a_times_b(t, ALL_SLOTS)
        pick_b(LAST)
        pick_a_times_b(LAST, HALVES[0])
        a_pick = keep.tile([P, HALF], F32, name="a_pick")
        nc.scalar.activation(out=a_pick[:], in_=xa_sb[LAST][:].indirect(entries(list_a, HALVES[1])), func=ACT.Copy)
        nc.vector.tensor_tensor(ab[:, LAST, HALVES[1]], a_pick[:], b_pick[LAST][:, HALVES[1]], ALU.mult)
        for h in range(2):
            quantise_u(h)

        old_sb = [
            keep.tile([P, 2, C], F32, name="old%d" % i, tag=tag) for i, tag in enumerate(("pick%d" % LAST, "products"))
        ]
        for i in range(2):
            nc.sync.dma_start(out=old_sb[i][:], in_=old_rows[:, 2 * i : 2 * i + 2, :])

        nc.scalar.copy(
            out=wb_sb[:].bitcast(U16).rearrange("p (t q) -> p t q", t=PACK),
            in_=wb_raw[:].bitcast(U16).rearrange("p (q t) -> p t q", t=PACK),
        )

        a_ps = [psum.tile([P, R], F32, name="a_ps%d" % h, tag="a%d" % h) for h in range(2)]
        h_ps = [psum.tile([P, PACK, HALF], F32, name="h_ps%d" % h) for h in range(2)]
        mags = tiles("mags", 2, [P, R], BF16)
        mean = tiles("mean", 2, [P, 1], F32)
        above = tiles("above", 2, [P, PACK, P], F32)
        h_codes = tiles("h_codes", 2, [P, HALF], U32)
        h_scales = tiles("h_scales", 2, [P, HALF], U8)
        p_sb = keep.tile([P, PACK, J], F32, name="p_sb")

        for h in range(2):
            nc.tensor.matmul_mx(
                out=a_ps[h][:],
                lhsT=u_codes[h][:].bitcast(E4M3),
                lhsT_scale=u_scales[h][:],
                rhs=w_sb[:].bitcast(E4M3),
                rhs_scale=ws_sb[:],
                start=True,
                stop=True,
            )
        wbs_sb = keep.tile([P, N], U8, name="wbs_sb", tag="scales0", align_bytes=64)
        nc.vector.tensor_copy(
            out=wbs_sb[:].rearrange("p (t q) -> p t q", t=PACK),
            in_=wbs_raw[:].rearrange("p (q t) -> p t q", t=PACK),
        )

        for h in range(2):
            nc.scalar.activation(out=mags[h][:], in_=a_ps[h][:], func=ACT.Abs, scale=1.0 / R, accum_out=mean[h][:])
        for h in range(2):
            for first in (0, 2):
                nc.vector.tensor_scalar(
                    out=above[h][:, first : first + 2, :],
                    in0=a_ps[h][:].rearrange("p (q t) -> p t q", t=PACK)[:, first : first + 2, :],
                    scalar1=mean[h][:],
                    scalar2=0.0,
                    op0=ALU.subtract,
                    op1=ALU.max,
                )
                for t in (first, first + 1):
                    nc.tensor.transpose(h_ps[h][:, t, :], above[h][:, t, :], ident[:])

        early_tags = (("p00", "p01"), ("p10", "a0"))
        p_early = [
            [psum.tile([P, HALF], F32, name="p%d%d" % (h, t), tag=early_tags[h][t]) for t in range(2)] for h in range(2)
        ]
        p_late = psum.tile([P, 2, J], F32, name="p_late")
        h16 = tiles("h16", 4, [P, QUARTER, PACK], BF16)

        def quantise_hid(h):
            for g in range(2):
                nc.vector.tensor_tensor(
                    h16[2 * h + g][:],
                    h_ps[h][:, :, g * QUARTER : (g + 1) * QUARTER].rearrange("p t j -> p j t"),
                    us_sb[:].to_broadcast([P, QUARTER, PACK]),
                    ALU.mult,
                )
            for g in range(2):
                cols = slice(g * QUARTER, (g + 1) * QUARTER)
                nc.vector.quantize_mx(
                    out=h_codes[h][:, cols].bitcast(E5M2),
                    scales=h_scales[h][:, cols],
                    in_=h16[2 * h + g][:].rearrange("p j t -> p (j t)"),
                )

        def second_product(h, t):
            nc.tensor.matmul_mx(
                out=p_early[h][t][:] if t < 2 else p_late[:, t - 2, HALVES[h]],
                lhsT=wb_sb[:, 2 * P * t : 2 * P * (t + 1)].bitcast(E2M1),
                lhsT_scale=wbs_sb[:, P * t : P * (t + 1)],
                rhs=h_codes[h][:].bitcast(E5M2),
                rhs_scale=h_scales[h][:],
                start=True,
                stop=True,
            )

        def put_on_scalar(t, slots):
            nc.scalar.activation(out=page[t][:].indirect(entries(list_c, slots)), in_=p_sb[:, t, slots], func=ACT.Copy)

        def put_on_vector(t, slots):
            nc.vector.tensor_copy(page[t][:].indirect(entries(list_c, slots)), p_sb[:, t, slots])

        for h, planes in enumerate(((1, 0, 2, 3), (0, 1, 2, 3))):
            quantise_hid(h)
            for t in planes:
                second_product(h, t)

        nc.scalar.copy(out=p_sb[:, 1, HALVES[0]], in_=p_early[0][1][:])
        put_on_scalar(1, HALVES[0])
        for h in range(2):
            nc.vector.tensor_copy(out=p_sb[:, 0, HALVES[h]], in_=p_early[h][0][:])
            put_on_vector(0, HALVES[h])
        nc.scalar.copy(out=p_sb[:, 1, HALVES[1]], in_=p_early[1][1][:])
        nc.scalar.copy(out=p_sb[:, 2:PACK, :], in_=p_late[:])
        put_on_scalar(1, HALVES[1])
        for t in (2, 3):
            put_on_scalar(t, ALL_SLOTS)

        y = keep.tile([P, PACK, C], F32, name="y")
        y16 = tiles("y16", CHUNKS, [P, CHUNK * PACK], BF16)
        y_codes = keep.tile([P, C], U32, name="y_codes", align_bytes=64)
        y_scales = keep.tile([P, C], U8, name="y_scales", align_bytes=64)
        out_words = out_1[0].rearrange("p c t -> p (c t)").bitcast(I32)

        def chunk_cols(first, count):
            return slice(first * CHUNK, (first + count) * CHUNK)

        def add_old(t, cols):
            nc.vector.scalar_tensor_tensor(
                out=y[:, t, cols],
                in0=old_sb[t // 2][:, t % 2, cols],
                scalar=0.5,
                in1=page[t][:, cols],
                op0=ALU.mult,
                op1=ALU.add,
            )

        for first in (0, CHUNKS // 2):
            cols = chunk_cols(first, CHUNKS // 2)
            add_old(0, cols)
            nc.sync.dma_start(out=out_rows[:, 0, cols], in_=y[:, 0, cols])
        for t in range(1, LAST):
            add_old(t, chunk_cols(0, CHUNKS))
            nc.sync.dma_start(out=out_rows[:, t, :], in_=y[:, t, :])
        for g in range(CHUNKS):
            add_old(LAST, chunk_cols(g, 1))
        nc.sync.dma_start(out=out_rows[:, LAST, :], in_=y[:, LAST, :])

        for g in range(CHUNKS):
            round_and_interleave = nc.scalar.copy if g in (0, CHUNKS - 1) else nc.vector.tensor_copy
            round_and_interleave(
                out=y16[g][:].rearrange("p (c i t) -> p c t i", i=RUN, t=PACK),
                in_=y[:, :, chunk_cols(g, 1)].rearrange("p t (c i) -> p c t i", i=RUN),
            )

        for first, count in ((0, 2), (2, 1), (3, 1)):
            for g in range(first, first + count):
                cols = chunk_cols(g, 1)
                nc.vector.quantize_mx(out=y_codes[:, cols].bitcast(E4M3), scales=y_scales[:, cols], in_=y16[g][:])
            cols = chunk_cols(first, count)
            nc.sync.dma_start(out=out_words[:, cols], in_=y_codes[:, cols].bitcast(I32))
        for q in range(QUADRANTS):
            queue = nc.sync if q % 2 == 0 else nc.scalar
            queue.dma_start(
                out=out_2[0, 4 * q : 4 * q + 4, :].bitcast(I32), in_=y_scales[scale_partitions(q), :].bitcast(I32)
            )
